import numpy as np
import ml_dtypes


def mxq(x, axis, fmt="e4m3"):
    dtype, down = {"e4m3": (ml_dtypes.float8_e4m3fn, 7), "e5m2": (ml_dtypes.float8_e5m2, 14)}[fmt]
    v = np.moveaxis(np.asarray(x, np.float32).astype(ml_dtypes.bfloat16).astype(np.float64), axis, -1)
    blocks = v.reshape(v.shape[:-1] + (-1, 32))
    amax = np.abs(blocks).max(-1, keepdims=True)
    byte = np.maximum(np.where(amax > 0, np.frexp(amax)[1] - 1 + 127, 0) - down, 1)
    scale = np.exp2(byte - 127.0)
    codes = (blocks / scale).astype(np.float32).astype(dtype).astype(np.float64)
    return np.moveaxis((codes * scale).reshape(v.shape), -1, axis)


WIDE = False


def mx_kscale(k):
    if not WIDE:
        return np.ones(k)
    levels = np.array([10, -10, 5, -5, 0])
    if k % 512:
        return np.exp2(np.random.permutation(np.resize(levels, k // 32))).repeat(32)
    a = np.empty((k // 512, 16))
    for p in range(k // 512):
        a[p, :8] = np.random.permutation(np.resize(levels, 8))
        for g in range(8):
            far = levels[np.abs(levels - a[p, g]) >= 10]
            a[p, g + 8] = far[np.random.randint(len(far))]
    return np.exp2(a.ravel()).repeat(32)


def f64(x):
    return np.asarray(x).astype(np.float64)


def striped(idx):
    return np.tile(idx.reshape(-1, 16).T, (8, 1)).astype(np.uint16)


def unstriped(offs):
    return offs[:16].T.reshape(-1).astype(np.int64)


def relu2(v):
    return np.maximum(v, 0.0) ** 2


K, T, S, N = 2048, 1024, 512, 128


def setup_inputs():
    n = np.random.standard_normal
    s = mx_kscale(K)[:, None]
    return {
        "xT": (n((K, S)) * s).astype(np.float32),
        "w": (n((K, N)) / np.sqrt(K) / s).astype(np.float32),
        "b": (0.3 * n((N, 1))).astype(np.float32),
        "gate": np.tile(np.random.uniform(0.2, 1.0, S), (N, 1)).astype(np.float32),
        "offs": striped(np.sort(np.random.permutation(T)[:S])),
    }


def reference(xT, w, b, gate, offs):
    idx = unstriped(offs)
    xq = mxq(f64(xT), 0, "e4m3")
    y = mxq(f64(w), 0, "e4m3").T @ xq
    y = relu2(y + f64(b))
    out = np.zeros((N, T))
    out[:, idx] = f64(gate) * y
    return out

@@ -1,0 +1,189 @@
+from contextlib import ExitStack
+
+import concourse.mybir as mybir
+
+K, T, S, N = 2048, 1024, 512, 128
+FLOPS = 2 * K * S * N
+
+F32 = mybir.dt.float32
+BF16 = mybir.dt.bfloat16
+U32 = mybir.dt.uint32
+U16 = mybir.dt.uint16
+U8 = mybir.dt.uint8
+FP8X4 = mybir.dt.float8_e4m3fn_x4
+ALU = mybir.AluOpType
+ACT = mybir.ActivationFunctionType
+
+P = 128
+PACK = 4
+K_PASS = P * PACK
+PASSES = K // K_PASS
+RUN = 4
+
+GROUPS = ((0, 128), (128, 256), (256, 384), (384, 512))
+LOADS = [
+    ("w", (0, 1, 2, 3), 0),
+    ("offs",),
+    ("x", 0, 256, 512, 256),
+    ("x", 1, 0, 512, 224),
+    ("x", 3, 256, 512, 144),
+    ("x", 2, 256, 512, 128),
+    ("x", 0, 0, 256, 64),
+    ("x", 2, 0, 128, 96),
+    ("x", 3, 0, 256, 192),
+    ("x", 2, 128, 256, 0),
+    ("gate", 0, 384),
+    ("gate", 384, 512),
+]
+VECTOR_EPILOGUE = ()
+STAGE_BUFS = 9
+DELAYS = [[2,3],[1,3],[1,0],[3,2]]
+
+
+def interleave(nc, grouped, raw, share):
+    width = raw.shape[2]
+    for copy, c0, c1 in ((nc.vector.tensor_copy, 0, share), (nc.scalar.copy, share, width)):
+        if c1 > c0:
+            copy(
+                out=grouped[:, c0:c1, :].rearrange("p (c i) t -> p c t i", i=RUN),
+                in_=raw[:, :, c0:c1].rearrange("p t (c i) -> p c t i", i=RUN),
+            )
+
+
+def tile_picked_place_lin_relu2_srt_l_kernel(tc, xT, w, b, gate, offs, out):
+    nc = tc.nc
+    with ExitStack() as ctx:
+        keep = ctx.enter_context(tc.tile_pool(name="keep", bufs=1))
+        psum = ctx.enter_context(tc.psum_pool(name="psum", bufs=1))
+
+        offsets = keep.tile([P, S // 16], U16, name="offsets")
+        bias = keep.tile([P, 1], F32, name="bias")
+        window = keep.tile([P, T], F32, name="window")
+        warm_in = keep.tile([P, 8], F32, name="warm_in")
+        warm_out = keep.tile([P, 8], F32, name="warm_out")
+
+        raws = {}
+        gates = {}
+        for i, load in enumerate(LOADS):
+            if load[0] == "w":
+                passes = load[1]
+                raw = keep.tile([P, len(passes), PACK, N], F32, name=f"raw{i}")
+                rows = w[passes[0] * K_PASS : (passes[-1] + 1) * K_PASS, :]
+                nc.sync.dma_start(
+                    out=raw[:].rearrange("p g t n -> p g (t n)"),
+                    in_=rows.rearrange("(g p t) n -> p g (t n)", p=P, t=PACK),
+                )
+                raws[i] = raw
+            elif load[0] == "x":
+                g, c0, c1 = load[1:4]
+                raw = keep.tile([P, PACK, c1 - c0], F32, name=f"raw{i}")
+                rows = xT[g * K_PASS : (g + 1) * K_PASS, c0:c1]
+                nc.sync.dma_start(out=raw[:], in_=rows.rearrange("(p t) c -> p t c", t=PACK))
+                raws[i] = raw
+            elif load[0] == "gate":
+                c0, c1 = load[1:3]
+                part = keep.tile([P, c1 - c0], F32, name=f"gate{i}")
+                nc.sync.dma_start(out=part[:], in_=gate[:, c0:c1])
+                for j, (g0, g1) in enumerate(GROUPS):
+                    if c0 <= g0 and g1 <= c1:
+                        gates[j] = part[:, g0 - c0 : g1 - c0]
+            else:
+                nc.sync.dma_start(offsets[:], offs)
+            if i == 0:
+                nc.scalar.dma_start(out=bias[:], in_=b)
+
+        nc.vector.memset(warm_in[:], 0.0)
+        nc.scalar.activation(out=warm_out[:], in_=warm_in[:], func=ACT.Square)
+        nc.vector.memset(window[:], 0.0)
+
+        sums = [psum.tile([P, c1 - c0], F32, name=f"sums{j}") for j, (c0, c1) in enumerate(GROUPS)]
+        done = [0] * len(GROUPS)
+        weights = {}
+        stages = [keep.tile([P, S, PACK], BF16, name=f"stage{r}", align_bytes=64) for r in range(STAGE_BUFS)]
+        turn = 0
+        waiting = []
+        later = []
+
+        def multiply(g, j, codes, scales):
+            g0, g1 = GROUPS[j]
+            nc.tensor.matmul_mx(
+                out=sums[j][:],
+                lhsT=weights[g][0].bitcast(FP8X4),
+                lhsT_scale=weights[g][1],
+                rhs=codes.bitcast(FP8X4),
+                rhs_scale=scales,
+                start=(done[j] == 0),
+                stop=(done[j] == PASSES - 1),
+            )
+            done[j] += 1
+            if done[j] == PASSES:
+                later.append([DELAYS[j][0], activate, j])
+                later.append([DELAYS[j][0] + DELAYS[j][1], scatter, j])
+
+        factors = {}
+
+        def activate(j):
+            g0, g1 = GROUPS[j]
+            relu = keep.tile([P, g1 - g0], F32, name=f"relu{j}")
+            other = keep.tile([P, g1 - g0], F32, name=f"other{j}")
+            if j in VECTOR_EPILOGUE:
+                nc.vector.tensor_scalar(
+                    out=relu[:], in0=sums[j][:], scalar1=bias[:], scalar2=0.0, op0=ALU.add, op1=ALU.max
+                )
+                nc.vector.scalar_tensor_tensor(
+                    out=other[:], in0=sums[j][:], scalar=bias[:], in1=gates[j], op0=ALU.add, op1=ALU.mult
+                )
+                factors[j] = (relu[:], other[:])
+            else:
+                nc.scalar.activation(out=relu[:], in_=sums[j][:], func=ACT.Relu, bias=bias[:])
+                nc.scalar.activation(out=other[:], in_=relu[:], func=ACT.Square)
+                factors[j] = (other[:], gates[j])
+
+        def scatter(j):
+            g0, g1 = GROUPS[j]
+            places = window[:].indirect(offsets[:, g0 // 16 : g1 // 16])
+            nc.vector.tensor_tensor(places, factors[j][0], factors[j][1], ALU.mult)
+
+        def flush(everything):
+            for entry in sorted(later, key=lambda entry: entry[0]):
+                if entry[0] > 0 and not everything:
+                    entry[0] -= 1
+                else:
+                    entry[1](entry[2])
+                    later.remove(entry)
+
+        for i, load in enumerate(LOADS):
+            if i not in raws:
+                continue
+            share = load[-1]
+            width = len(load[1]) * N if load[0] == "w" else load[3] - load[2]
+            grouped = stages[turn % STAGE_BUFS][:, 0:width, :]
+            turn += 1
+            codes = keep.tile([P, width], U32, name=f"codes{i}", align_bytes=64)
+            scales = keep.tile([P, width], U8, name=f"scales{i}", align_bytes=64)
+            if load[0] == "w":
+                for s in range(len(load[1])):
+                    part = min(max(share - s * N, 0), N)
+                    interleave(nc, grouped[:, s * N : (s + 1) * N, :], raws[i][:, s, :, :], part)
+            else:
+                interleave(nc, grouped, raws[i][:], share)
+            nc.vector.quantize_mx(
+                out=codes[:].bitcast(FP8X4),
+                scales=scales[:],
+                in_=grouped.rearrange("p c t -> p (c t)"),
+            )
+            if load[0] == "w":
+                for s, g in enumerate(load[1]):
+                    weights[g] = (codes[:, s * N : (s + 1) * N], scales[:, s * N : (s + 1) * N])
+            else:
+                g, c0, c1 = load[1:4]
+                for j, (g0, g1) in enumerate(GROUPS):
+                    if c0 <= g0 and g1 <= c1:
+                        waiting.append((g, j, codes[:, g0 - c0 : g1 - c0], scales[:, g0 - c0 : g1 - c0]))
+            for item in [item for item in waiting if item[0] in weights]:
+                multiply(*item)
+            waiting = [item for item in waiting if item[0] not in weights]
+            flush(False)
+        flush(True)
+
+        nc.sync.dma_start(out=out, in_=window[:])

@@ -22,22 +22,20 @@ RUN = 4
 
 GROUPS = ((0, 128), (128, 256), (256, 384), (384, 512))
 LOADS = [
-    ("w", (0, 1, 2, 3), 0),
+    ("x", 1, 0, 512, ((512, 496),)),
+    ("x", 2, 0, 512, ((128, 128), (256, 64), (128, 0))),
+    ("w", (1, 2, 3), ((128, 128), (256, 256))),
+    ("x", 0, 0, 512, ((128, 0), (256, 256), (128, 112))),
+    ("w", (0,), ((128, 0),)),
+    ("x", 3, 0, 256, ((128, 128), (128, 48))),
+    ("x", 3, 256, 384, ((128, 80),)),
+    ("x", 3, 384, 512, ((128, 128),)),
     ("offs",),
-    ("x", 0, 256, 512, 256),
-    ("x", 1, 0, 512, 224),
-    ("x", 3, 256, 512, 144),
-    ("x", 2, 256, 512, 128),
-    ("x", 0, 0, 256, 64),
-    ("x", 2, 0, 128, 96),
-    ("x", 3, 0, 256, 192),
-    ("x", 2, 128, 256, 0),
-    ("gate", 0, 384),
-    ("gate", 384, 512),
+    ("gate", 0, 256),
+    ("gate", 256, 512),
 ]
-VECTOR_EPILOGUE = ()
-STAGE_BUFS = 9
-DELAYS = [[2,3],[1,3],[1,0],[3,2]]
+DELAYS = [[2,3],[1,0],[2,2],[1,0]]
+MERGED = [2,0]
 
 
 def interleave(nc, grouped, raw, share):
@@ -57,13 +55,16 @@ def tile_picked_place_lin_relu2_srt_l_kernel(tc, xT, w, b, gate, offs, out):
         psum = ctx.enter_context(tc.psum_pool(name="psum", bufs=1))
 
         offsets = keep.tile([P, S // 16], U16, name="offsets")
-        bias = keep.tile([P, 1], F32, name="bias")
+        bias_rows = keep.tile([P, 32], F32, name="bias_rows", align_bytes=64)
+        bias_cols = keep.tile([P, 32], F32, name="bias_cols", align_bytes=64)
+        bias = bias_cols[:, 0:1]
+        nc.vector.memset(bias_rows[:], 0.0)
         window = keep.tile([P, T], F32, name="window")
         warm_in = keep.tile([P, 8], F32, name="warm_in")
         warm_out = keep.tile([P, 8], F32, name="warm_out")
 
         raws = {}
-        gates = {}
+        gates = keep.tile([P, S], F32, name="gates")
         for i, load in enumerate(LOADS):
             if load[0] == "w":
                 passes = load[1]
@@ -82,24 +83,20 @@ def tile_picked_place_lin_relu2_srt_l_kernel(tc, xT, w, b, gate, offs, out):
                 raws[i] = raw
             elif load[0] == "gate":
                 c0, c1 = load[1:3]
-                part = keep.tile([P, c1 - c0], F32, name=f"gate{i}")
-                nc.sync.dma_start(out=part[:], in_=gate[:, c0:c1])
-                for j, (g0, g1) in enumerate(GROUPS):
-                    if c0 <= g0 and g1 <= c1:
-                        gates[j] = part[:, g0 - c0 : g1 - c0]
+                nc.sync.dma_start(out=gates[:, c0:c1], in_=gate[:, c0:c1])
             else:
                 nc.sync.dma_start(offsets[:], offs)
             if i == 0:
-                nc.scalar.dma_start(out=bias[:], in_=b)
+                nc.sync.dma_start(out=bias_rows[0:P:32, :], in_=b.rearrange("(q i) one -> q (i one)", i=32))
 
         nc.vector.memset(warm_in[:], 0.0)
         nc.scalar.activation(out=warm_out[:], in_=warm_in[:], func=ACT.Square)
         nc.vector.memset(window[:], 0.0)
+        nc.vector.transpose(bias_cols[:], bias_rows[:])
 
         sums = [psum.tile([P, c1 - c0], F32, name=f"sums{j}") for j, (c0, c1) in enumerate(GROUPS)]
         done = [0] * len(GROUPS)
         weights = {}
-        stages = [keep.tile([P, S, PACK], BF16, name=f"stage{r}", align_bytes=64) for r in range(STAGE_BUFS)]
         turn = 0
         waiting = []
         later = []
@@ -121,28 +118,34 @@ def tile_picked_place_lin_relu2_srt_l_kernel(tc, xT, w, b, gate, offs, out):
                 later.append([DELAYS[j][0] + DELAYS[j][1], scatter, j])
 
         factors = {}
+        ready = set()
+
+        def run_of(j):
+            run = [j]
+            while run[0] - 1 in MERGED:
+                run = [run[0] - 1] + run
+            while run[-1] in MERGED:
+                run = run + [run[-1] + 1]
+            return run
 
         def activate(j):
             g0, g1 = GROUPS[j]
             relu = keep.tile([P, g1 - g0], F32, name=f"relu{j}")
-            other = keep.tile([P, g1 - g0], F32, name=f"other{j}")
-            if j in VECTOR_EPILOGUE:
-                nc.vector.tensor_scalar(
-                    out=relu[:], in0=sums[j][:], scalar1=bias[:], scalar2=0.0, op0=ALU.add, op1=ALU.max
-                )
-                nc.vector.scalar_tensor_tensor(
-                    out=other[:], in0=sums[j][:], scalar=bias[:], in1=gates[j], op0=ALU.add, op1=ALU.mult
-                )
-                factors[j] = (relu[:], other[:])
-            else:
-                nc.scalar.activation(out=relu[:], in_=sums[j][:], func=ACT.Relu, bias=bias[:])
-                nc.scalar.activation(out=other[:], in_=relu[:], func=ACT.Square)
-                factors[j] = (other[:], gates[j])
+            first = run_of(j)[0]
+            if first not in factors:
+                width = GROUPS[run_of(j)[-1]][1] - GROUPS[first][0]
+                factors[first] = keep.tile([P, width], F32, name=f"other{first}")
+            other = factors[first][:, g0 - GROUPS[first][0] : g1 - GROUPS[first][0]]
+            nc.scalar.activation(out=relu[:], in_=sums[j][:], func=ACT.Relu, bias=bias)
+            nc.scalar.activation(out=other, in_=relu[:], func=ACT.Square)
 
         def scatter(j):
-            g0, g1 = GROUPS[j]
-            places = window[:].indirect(offsets[:, g0 // 16 : g1 // 16])
-            nc.vector.tensor_tensor(places, factors[j][0], factors[j][1], ALU.mult)
+            ready.add(j)
+            run = run_of(j)
+            if all(member in ready for member in run):
+                g0, g1 = GROUPS[run[0]][0], GROUPS[run[-1]][1]
+                places = window[:].indirect(offsets[:, g0 // 16 : g1 // 16])
+                nc.vector.tensor_tensor(places, factors[run[0]][:], gates[:, g0:g1], ALU.mult)
 
         def flush(everything):
             for entry in sorted(later, key=lambda entry: entry[0]):
@@ -155,35 +158,37 @@ def tile_picked_place_lin_relu2_srt_l_kernel(tc, xT, w, b, gate, offs, out):
         for i, load in enumerate(LOADS):
             if i not in raws:
                 continue
-            share = load[-1]
-            width = len(load[1]) * N if load[0] == "w" else load[3] - load[2]
-            grouped = stages[turn % STAGE_BUFS][:, 0:width, :]
-            turn += 1
-            codes = keep.tile([P, width], U32, name=f"codes{i}", align_bytes=64)
-            scales = keep.tile([P, width], U8, name=f"scales{i}", align_bytes=64)
-            if load[0] == "w":
-                for s in range(len(load[1])):
-                    part = min(max(share - s * N, 0), N)
-                    interleave(nc, grouped[:, s * N : (s + 1) * N, :], raws[i][:, s, :, :], part)
-            else:
-                interleave(nc, grouped, raws[i][:], share)
-            nc.vector.quantize_mx(
-                out=codes[:].bitcast(FP8X4),
-                scales=scales[:],
-                in_=grouped.rearrange("p c t -> p (c t)"),
-            )
-            if load[0] == "w":
-                for s, g in enumerate(load[1]):
-                    weights[g] = (codes[:, s * N : (s + 1) * N], scales[:, s * N : (s + 1) * N])
-            else:
-                g, c0, c1 = load[1:4]
-                for j, (g0, g1) in enumerate(GROUPS):
-                    if c0 <= g0 and g1 <= c1:
-                        waiting.append((g, j, codes[:, g0 - c0 : g1 - c0], scales[:, g0 - c0 : g1 - c0]))
-            for item in [item for item in waiting if item[0] in weights]:
-                multiply(*item)
-            waiting = [item for item in waiting if item[0] not in weights]
-            flush(False)
+            first = 0
+            for width, share in load[-1]:
+                grouped = keep.tile([P, width, PACK], BF16, name=f"grouped{turn}", align_bytes=64)
+                grouped = grouped[:]
+                codes = keep.tile([P, width], U32, name=f"codes{turn}", align_bytes=64)
+                scales = keep.tile([P, width], U8, name=f"scales{turn}", align_bytes=64)
+                turn += 1
+                if load[0] == "w":
+                    for s in range(0, width, N):
+                        part = min(max(share - s, 0), N)
+                        interleave(nc, grouped[:, s : s + N, :], raws[i][:, (first + s) // N, :, :], part)
+                else:
+                    interleave(nc, grouped, raws[i][:, :, first : first + width], share)
+                nc.vector.quantize_mx(
+                    out=codes[:].bitcast(FP8X4),
+                    scales=scales[:],
+                    in_=grouped.rearrange("p c t -> p (c t)"),
+                )
+                if load[0] == "w":
+                    for s in range(0, width, N):
+                        weights[load[1][(first + s) // N]] = (codes[:, s : s + N], scales[:, s : s + N])
+                else:
+                    c0 = load[2] + first
+                    for j, (g0, g1) in enumerate(GROUPS):
+                        if c0 <= g0 and g1 <= c0 + width:
+                            waiting.append((load[1], j, codes[:, g0 - c0 : g1 - c0], scales[:, g0 - c0 : g1 - c0]))
+                for item in [item for item in waiting if item[0] in weights]:
+                    multiply(*item)
+                waiting = [item for item in waiting if item[0] not in weights]
+                flush(False)
+                first += width
         flush(True)
 
         nc.sync.dma_start(out=out, in_=window[:])

@@ -18,7 +18,7 @@ P = 128
 PACK = 4
 K_PASS = P * PACK
 PASSES = K // K_PASS
-RUN = 4
+RUN = 2
 
 GROUPS = ((0, 128), (128, 256), (256, 384), (384, 512))
 LOADS = [

from contextlib import ExitStack

import concourse.mybir as mybir

K, T, S, N = 2048, 1024, 512, 128
FLOPS = 2 * K * S * N

F32 = mybir.dt.float32
BF16 = mybir.dt.bfloat16
U32 = mybir.dt.uint32
U16 = mybir.dt.uint16
U8 = mybir.dt.uint8
FP8X4 = mybir.dt.float8_e4m3fn_x4
ALU = mybir.AluOpType
ACT = mybir.ActivationFunctionType

P = 128
PACK = 4
K_PASS = P * PACK
PASSES = K // K_PASS
RUN = 2

GROUPS = ((0, 128), (128, 256), (256, 384), (384, 512))
LOADS = [
    ("x", 1, 0, 512, ((512, 496),)),
    ("x", 2, 0, 512, ((128, 128), (256, 64), (128, 0))),
    ("w", (1, 2, 3), ((128, 128), (256, 256))),
    ("x", 0, 0, 512, ((128, 0), (256, 256), (128, 112))),
    ("w", (0,), ((128, 0),)),
    ("x", 3, 0, 256, ((128, 128), (128, 48))),
    ("x", 3, 256, 384, ((128, 80),)),
    ("x", 3, 384, 512, ((128, 128),)),
    ("offs",),
    ("gate", 0, 256),
    ("gate", 256, 512),
]
DELAYS = [[2,3],[1,0],[2,2],[1,0]]
MERGED = [2,0]


def interleave(nc, grouped, raw, share):
    width = raw.shape[2]
    for copy, c0, c1 in ((nc.vector.tensor_copy, 0, share), (nc.scalar.copy, share, width)):
        if c1 > c0:
            copy(
                out=grouped[:, c0:c1, :].rearrange("p (c i) t -> p c t i", i=RUN),
                in_=raw[:, :, c0:c1].rearrange("p t (c i) -> p c t i", i=RUN),
            )


def tile_picked_place_lin_relu2_srt_l_kernel(tc, xT, w, b, gate, offs, out):
    nc = tc.nc
    with ExitStack() as ctx:
        keep = ctx.enter_context(tc.tile_pool(name="keep", bufs=1))
        psum = ctx.enter_context(tc.psum_pool(name="psum", bufs=1))

        offsets = keep.tile([P, S // 16], U16, name="offsets")
        bias_rows = keep.tile([P, 32], F32, name="bias_rows", align_bytes=64)
        bias_cols = keep.tile([P, 32], F32, name="bias_cols", align_bytes=64)
        bias = bias_cols[:, 0:1]
        nc.vector.memset(bias_rows[:], 0.0)
        window = keep.tile([P, T], F32, name="window")
        warm_in = keep.tile([P, 8], F32, name="warm_in")
        warm_out = keep.tile([P, 8], F32, name="warm_out")

        raws = {}
        gates = keep.tile([P, S], F32, name="gates")
        for i, load in enumerate(LOADS):
            if load[0] == "w":
                passes = load[1]
                raw = keep.tile([P, len(passes), PACK, N], F32, name=f"raw{i}")
                rows = w[passes[0] * K_PASS : (passes[-1] + 1) * K_PASS, :]
                nc.sync.dma_start(
                    out=raw[:].rearrange("p g t n -> p g (t n)"),
                    in_=rows.rearrange("(g p t) n -> p g (t n)", p=P, t=PACK),
                )
                raws[i] = raw
            elif load[0] == "x":
                g, c0, c1 = load[1:4]
                raw = keep.tile([P, PACK, c1 - c0], F32, name=f"raw{i}")
                rows = xT[g * K_PASS : (g + 1) * K_PASS, c0:c1]
                nc.sync.dma_start(out=raw[:], in_=rows.rearrange("(p t) c -> p t c", t=PACK))
                raws[i] = raw
            elif load[0] == "gate":
                c0, c1 = load[1:3]
                nc.sync.dma_start(out=gates[:, c0:c1], in_=gate[:, c0:c1])
            else:
                nc.sync.dma_start(offsets[:], offs)
            if i == 0:
                nc.sync.dma_start(out=bias_rows[0:P:32, :], in_=b.rearrange("(q i) one -> q (i one)", i=32))

        nc.vector.memset(warm_in[:], 0.0)
        nc.scalar.activation(out=warm_out[:], in_=warm_in[:], func=ACT.Square)
        nc.vector.memset(window[:], 0.0)
        nc.vector.transpose(bias_cols[:], bias_rows[:])

        sums = [psum.tile([P, c1 - c0], F32, name=f"sums{j}") for j, (c0, c1) in enumerate(GROUPS)]
        done = [0] * len(GROUPS)
        weights = {}
        turn = 0
        waiting = []
        later = []

        def multiply(g, j, codes, scales):
            g0, g1 = GROUPS[j]
            nc.tensor.matmul_mx(
                out=sums[j][:],
                lhsT=weights[g][0].bitcast(FP8X4),
                lhsT_scale=weights[g][1],
                rhs=codes.bitcast(FP8X4),
                rhs_scale=scales,
                start=(done[j] == 0),
                stop=(done[j] == PASSES - 1),
            )
            done[j] += 1
            if done[j] == PASSES:
                later.append([DELAYS[j][0], activate, j])
                later.append([DELAYS[j][0] + DELAYS[j][1], scatter, j])

        factors = {}
        ready = set()

        def run_of(j):
            run = [j]
            while run[0] - 1 in MERGED:
                run = [run[0] - 1] + run
            while run[-1] in MERGED:
                run = run + [run[-1] + 1]
            return run

        def activate(j):
            g0, g1 = GROUPS[j]
            relu = keep.tile([P, g1 - g0], F32, name=f"relu{j}")
            first = run_of(j)[0]
            if first not in factors:
                width = GROUPS[run_of(j)[-1]][1] - GROUPS[first][0]
                factors[first] = keep.tile([P, width], F32, name=f"other{first}")
            other = factors[first][:, g0 - GROUPS[first][0] : g1 - GROUPS[first][0]]
            nc.scalar.activation(out=relu[:], in_=sums[j][:], func=ACT.Relu, bias=bias)
            nc.scalar.activation(out=other, in_=relu[:], func=ACT.Square)

        def scatter(j):
            ready.add(j)
            run = run_of(j)
            if all(member in ready for member in run):
                g0, g1 = GROUPS[run[0]][0], GROUPS[run[-1]][1]
                places = window[:].indirect(offsets[:, g0 // 16 : g1 // 16])
                nc.vector.tensor_tensor(places, factors[run[0]][:], gates[:, g0:g1], ALU.mult)

        def flush(everything):
            for entry in sorted(later, key=lambda entry: entry[0]):
                if entry[0] > 0 and not everything:
                    entry[0] -= 1
                else:
                    entry[1](entry[2])
                    later.remove(entry)

        for i, load in enumerate(LOADS):
            if i not in raws:
                continue
            first = 0
            for width, share in load[-1]:
                grouped = keep.tile([P, width, PACK], BF16, name=f"grouped{turn}", align_bytes=64)
                grouped = grouped[:]
                codes = keep.tile([P, width], U32, name=f"codes{turn}", align_bytes=64)
                scales = keep.tile([P, width], U8, name=f"scales{turn}", align_bytes=64)
                turn += 1
                if load[0] == "w":
                    for s in range(0, width, N):
                        part = min(max(share - s, 0), N)
                        interleave(nc, grouped[:, s : s + N, :], raws[i][:, (first + s) // N, :, :], part)
                else:
                    interleave(nc, grouped, raws[i][:, :, first : first + width], share)
                nc.vector.quantize_mx(
                    out=codes[:].bitcast(FP8X4),
                    scales=scales[:],
                    in_=grouped.rearrange("p c t -> p (c t)"),
                )
                if load[0] == "w":
                    for s in range(0, width, N):
                        weights[load[1][(first + s) // N]] = (codes[:, s : s + N], scales[:, s : s + N])
                else:
                    c0 = load[2] + first
                    for j, (g0, g1) in enumerate(GROUPS):
                        if c0 <= g0 and g1 <= c0 + width:
                            waiting.append((load[1], j, codes[:, g0 - c0 : g1 - c0], scales[:, g0 - c0 : g1 - c0]))
                for item in [item for item in waiting if item[0] in weights]:
                    multiply(*item)
                waiting = [item for item in waiting if item[0] not in weights]
                flush(False)
                first += width
        flush(True)

        nc.sync.dma_start(out=out, in_=window[:])
